import numpy as np, ml_dtypes
CORES = [44,45,46,47,172,173,174,175,300,301,302,303,428,429,430,431]
N = 16
F, TK = 32, 128
def setup_inputs(rng):
    return {"x": rng.standard_normal((N, 128, N * TK), dtype=np.float32).astype(ml_dtypes.bfloat16), "w": rng.standard_normal((N, 128, F), dtype=np.float32).astype(ml_dtypes.bfloat16)}
def setup_inputs_big(rng):
    d = setup_inputs(rng)
    for k in ("x", "w"): d[k] = (d[k].astype(np.float32) * 1024.0).astype(d[k].dtype)
    return d
def setup_inputs_small(rng):
    d = setup_inputs(rng)
    for k in ("x", "w"): d[k] = (d[k].astype(np.float32) * (1 / 1024.0)).astype(d[k].dtype)
    return d
def reference(x, w):
    X, W = x.astype(np.float64), w.astype(np.float64)
    y = np.zeros((N, F, N * TK))
    for r in range(N):
        for j in range(N):
            y[r][:, TK * j:TK * j + TK] = W[r].T @ X[j][:, TK * r:TK * r + TK]
    return {"y": y.astype(ml_dtypes.bfloat16 if x.dtype != np.float64 else np.float64)}

@@ -1,0 +1,250 @@
+from concourse.bass import DstId, RemoteDMATransfer
+
+TK, F = 128, 32
+ZP = 136
+SWITCH_FIRST = (0, 1, 2, 3)
+
+SCRATCH = {
+    "xs": ("sbuf", [128, 16 * TK], "bfloat16"),
+    "ws": ("sbuf", [128, F], "bfloat16"),
+    "wl": ("sbuf", [128, 4 * F], "bfloat16"),
+    "z": ("sbuf", [128, 4 * ZP], "bfloat16"),
+    "xl": ("sbuf", [128, 16 * TK], "bfloat16"),
+    "res": ("sbuf", [128, 4 * TK], "bfloat16"),
+    "p0": ("psum", [128, 512], "float32"),
+    "p1": ("psum", [128, 512], "float32"),
+    "p2": ("psum", [128, 512], "float32"),
+    "p3": ("psum", [128, 512], "float32"),
+    "yl": ("dram", [4, 128, TK], "bfloat16"),
+}
+SEMAPHORES = ["ldw", "ld0", "ld1", "ld2", "ld3", "ms", "w", "z", "x0", "x1", "x2", "x3",
+              "mm0", "mm1", "mm2", "mm3", "cp", "y0", "y1", "y2", "y3", "st", "sent"]
+
+
+def _bits(mask):
+    return [e for e in range(mask.bit_length()) if (mask >> e) & 1]
+
+
+def _mk(engines):
+    m = 0
+    for e in engines:
+        m |= 1 << e
+    return m
+
+
+def _plan(T, topo):
+    cores = list(T.cores)
+    rank = {c: i for i, c in enumerate(cores)}
+    hosts = []
+    for c in cores:
+        if topo.host(c) not in hosts:
+            hosts.append(topo.host(c))
+    mem = {h: [c for c in cores if topo.host(c) == h] for h in hosts}
+    nq = len(mem[hosts[0]])
+    sw, cb, dg = {}, {}, {}
+    for h in hosts:
+        for k in hosts:
+            if k == h:
+                continue
+            a, b = mem[h][0], mem[k][0]
+            if not topo.may_write(a, b):
+                dg[h] = k
+            elif topo.same_plane(a, b):
+                sw[h] = k
+            else:
+                cb[h] = k
+
+    def same_chip(a, b):
+        return topo.host(a) == topo.host(b) and topo.chip(a) == topo.chip(b)
+
+    jobs = {}
+    for h in hosts:
+        m = mem[h]
+        base = m[0] - m[0] % topo.CORES_PER_HOST
+        mate = [x for x in range(base, base + topo.CORES_PER_HOST) if topo.mates(m[0], x)][0]
+        own = [c for c in m if topo.may_write(c, mate)]
+        oth = [c for c in m if not topo.may_write(c, mate)]
+        if len(own) != len(oth):
+            own, oth = m[0::2], m[1::2]
+        c_c, c_s, c_r, c_o = own[0], own[1], oth[0], oth[1]
+        jobs[c_o] = [(mem[h][q], h) for q in range(nq)]
+        jobs[c_s] = [(mem[sw[h]][q], h) for q in range(nq)]
+        jobs[c_c] = [(mem[cb[h]][q], h) for q in range(nq)]
+        jobs[c_r] = [(mem[cb[h]][q], sw[h]) if q in SWITCH_FIRST else (mem[sw[h]][q], cb[h]) for q in range(nq)]
+    handler = {}
+    for c in cores:
+        for k, (d, hs) in enumerate(jobs[c]):
+            handler[(d, hs)] = (c, k)
+
+    plan = {c: {"jobs": jobs[c], "w_expect": 0, "x_expect": [0] * nq, "y_expect": [0] * len(hosts),
+                "self_w": None, "self_res": None} for c in cores}
+    for c in cores:
+        p = plan[c]
+        h = topo.host(c)
+        a = mem[h].index(c)
+        far = [d for d in cores if not same_chip(c, d) and topo.may_write(c, d)][0]
+        near = [d for d in cores if d != c and same_chip(c, d)][0]
+        off = _bits(topo.mask(c, far))
+        on = _bits(topo.mask(c, near))
+        hi = [e for e in on if e not in off]
+        half = len(off) // 2
+
+        wd = [handler[(c, hs)] for hs in hosts]
+        for rc, k in wd:
+            if rc == c:
+                p["self_w"] = k
+            else:
+                plan[rc]["w_expect"] += len(off)
+        p["wsend"] = (_mk(off), [(rc, k) for rc, k in wd if rc != c])
+
+        msgs = []
+        for hd in hosts:
+            q = 0
+            while q < nq:
+                rc, k = handler[(mem[hd][q], h)]
+                n = 1
+                while q + n < nq and handler[(mem[hd][q + n], h)] == (rc, k + n):
+                    n += 1
+                msgs.append((rc, TK * rank[mem[hd][q]], TK * n, a * nq * TK + TK * k, hosts.index(hd)))
+                q += n
+        offm = [m for m in msgs if not same_chip(c, m[0])]
+        onm = [m for m in msgs if m[0] != c and same_chip(c, m[0])]
+        selfm = [m for m in msgs if m[0] == c]
+        if len(onm) <= 2:
+            on_sets, pool = [hi[:half], hi[half:]], off
+        else:
+            on_sets, pool = [hi[:half], hi[half:], off[half:]], (off[:half] if len(offm) == 1 else off)
+        per = len(pool) // len(offm)
+        sends = [(m, pool[i * per:(i + 1) * per]) for i, m in enumerate(offm)]
+        sends += [(m, on_sets[i]) for i, m in enumerate(onm)]
+        calls = []
+        for m, engines in sends:
+            plan[m[0]]["x_expect"][a] += len(engines)
+            hit = [cl for cl in calls if cl[0] == m[2]]
+            if not hit:
+                hit = [(m[2], [])]
+                calls.append(hit[0])
+            hit[0][1].append((m, _mk(engines)))
+        p["xcalls"] = [cl[1] for cl in calls]
+        order = []
+        for m in offm + onm + selfm:
+            if m[4] not in order:
+                order.append(m[4])
+        p["loads"] = order
+        p["slab_col"] = [TK * rank[mem[hd][0]] for hd in hosts]
+        p["self_slabs"] = [m[4] for m in selfm]
+
+        rhs = []
+        for k, (d, hs) in enumerate(jobs[c]):
+            rhs.append([("xs", TK * rank[d]) if mem[hs][s] == c else ("xl", s * nq * TK + TK * k)
+                        for s in range(nq)])
+        p["rhs"] = rhs
+        p["a_order"] = ([a] if selfm else []) + [s for s in range(nq) if not (selfm and s == a)]
+        p["a_self"] = a if selfm else None
+
+        outs = [(d, k, hosts.index(hs)) for k, (d, hs) in enumerate(jobs[c]) if d != c]
+        for k, (d, hs) in enumerate(jobs[c]):
+            if d == c:
+                p["self_res"] = (k, hosts.index(hs))
+        pool = on if all(same_chip(c, d) for d, k, s in outs) else off
+        per = 1
+        while per * 2 * len(outs) <= len(pool):
+            per *= 2
+        p["rsend"] = []
+        for i, (d, k, s) in enumerate(outs):
+            p["rsend"].append((d, k, s, _mk(pool[i * per:(i + 1) * per])))
+            plan[d]["y_expect"][s] += per
+        p["stores"] = [hosts.index(x) for x in (h, sw[h], cb[h], dg[h])]
+    return plan
+
+
+def rank_program(g, core, T, topo):
+    if T.rank_of(core) is None:
+        return
+    p = _plan(T, topo)[core]
+    S = T.sem
+    nq = len(p["jobs"])
+    slab = nq * TK
+
+    def dst_id(d):
+        rid, pid = topo.addr(d, core)
+        return DstId(rid=rid, pnc=pid)
+
+    g.sync.dma_start(T.ws[:], T.w[:]).then_inc(S.ldw, 16)
+    for i, s in enumerate(p["loads"]):
+        q = g.scalar if i % 2 == 0 else g.sync
+        c0 = p["slab_col"][s]
+        q.dma_start(T.xs[:, c0:c0 + slab], T.x[:, c0:c0 + slab]).then_inc(S["ld%d" % s], 16)
+
+    sent = 0
+    mask, dests = p["wsend"]
+    g.wait_ge(S.ldw, 16)
+    g.remote_dma_fused([RemoteDMATransfer(dst_ids=[dst_id(d) for d, k in dests], dma_engine_mask=mask, remote_sem=S.w,
+                                          srcs=[T.ws[:]], dsts=[T.wl[:, F * k:F * k + F] for d, k in dests])],
+                       local_sem=S.sent)
+    sent += len(_bits(mask))
+
+    a_me = None
+    waited = []
+    for call in p["xcalls"]:
+        trs = []
+        for (d, c0, width, d0, s), mask in call:
+            if s not in waited:
+                g.wait_ge(S["ld%d" % s], 16)
+                waited.append(s)
+            a_me = d0 // slab
+            trs.append(RemoteDMATransfer(dst_ids=[dst_id(d)], dma_engine_mask=mask, remote_sem=S["x%d" % a_me],
+                                         src=T.xs[:, c0:c0 + width], dst=T.xl[:, d0:d0 + width]))
+            sent += len(_bits(mask))
+        g.remote_dma_fused(trs, local_sem=S.sent)
+
+    v = g.vector
+    v.memset(T.z[:], 0.0).then_inc(S.ms, 1)
+    v.wait_ge(S.ms, 1)
+    v.wait_ge(S.w, p["w_expect"])
+    if p["self_w"] is not None:
+        v.wait_ge(S.ldw, 16)
+    for k in range(nq):
+        src = T.ws[:] if k == p["self_w"] else T.wl[:, F * k:F * k + F]
+        v.tensor_copy(T.z[:, ZP * k + 3:ZP * k + 3 + 4 * F:4], src).then_inc(S.z, 1)
+
+    t = g.tensor
+    t.wait_ge(S.z, nq)
+    order = p["a_order"]
+    for i, a in enumerate(order):
+        if a == p["a_self"]:
+            for s in p["self_slabs"]:
+                t.wait_ge(S["ld%d" % s], 16)
+        else:
+            t.wait_ge(S["x%d" % a], p["x_expect"][a])
+        for k in range(nq):
+            name, c0 = p["rhs"][k][a]
+            mm = t.matmul(T["p%d" % k][:, 0:TK], T.z[:, ZP * k + 3 - a:ZP * k + 3 - a + 128], T[name][:, c0:c0 + TK],
+                          i == 0, i == len(order) - 1)
+            if i == len(order) - 1:
+                mm.then_inc(S["mm%d" % k], 1)
+
+    for k in range(nq):
+        v.wait_ge(S["mm%d" % k], 1)
+        v.tensor_copy(T.res[:, TK * k:TK * k + TK], T["p%d" % k][:, 0:TK]).then_inc(S.cp, 1)
+    g.wait_ge(S.cp, nq)
+    trs = []
+    for d, k, s, mask in p["rsend"]:
+        trs.append(RemoteDMATransfer(dst_ids=[dst_id(d)], dma_engine_mask=mask, remote_sem=S["y%d" % s],
+                                     src=T.res[:, TK * k:TK * k + TK], dst=T.yl[s]))
+        sent += len(_bits(mask))
+    g.remote_dma_fused(trs, local_sem=S.sent)
+
+    for i, s in enumerate(p["stores"]):
+        q = g.sync if i in (0, 3) else g.scalar
+        c0 = p["slab_col"][s]
+        if p["self_res"] is not None and p["self_res"][1] == s:
+            k = p["self_res"][0]
+            q.wait_ge(S.cp, nq)
+            q.dma_start(T.y[:, c0:c0 + slab], T.res[:, TK * k:TK * k + TK]).then_inc(S.st, 16)
+        else:
+            q.wait_ge(S["y%d" % s], p["y_expect"][s])
+            q.dma_start(T.y[:, c0:c0 + slab], T.yl[s]).then_inc(S.st, 16)
+
+    g.wait_ge(S.sent, sent)
+    g.wait_ge(S.st, 16 * len(p["stores"]))

@@ -2,7 +2,6 @@ from concourse.bass import DstId, RemoteDMATransfer
 
 TK, F = 128, 32
 ZP = 136
-SWITCH_FIRST = (0, 1, 2, 3)
 
 SCRATCH = {
     "xs": ("sbuf", [128, 16 * TK], "bfloat16"),
@@ -17,8 +16,9 @@ SCRATCH = {
     "p3": ("psum", [128, 512], "float32"),
     "yl": ("dram", [4, 128, TK], "bfloat16"),
 }
-SEMAPHORES = ["ldw", "ld0", "ld1", "ld2", "ld3", "ms", "w", "z", "x0", "x1", "x2", "x3",
-              "mm0", "mm1", "mm2", "mm3", "cp", "y0", "y1", "y2", "y3", "st", "sent"]
+SEMAPHORES = ["ldw", "ld0", "ld1", "ld2", "ld3", "ms", "w", "z", "x0_0", "x0_1", "x0_2", "x0_3",
+              "x1_0", "x1_1", "x1_2", "x1_3", "mm0", "mm1", "mm2", "mm3", "cp0", "cp1",
+              "y0", "y1", "y2", "y3", "st", "sent"]
 
 
 def _bits(mask):
@@ -57,7 +57,7 @@ def _plan(T, topo):
     def same_chip(a, b):
         return topo.host(a) == topo.host(b) and topo.chip(a) == topo.chip(b)
 
-    jobs = {}
+    jobs, groups = {}, {}
     for h in hosts:
         m = mem[h]
         base = m[0] - m[0] % topo.CORES_PER_HOST
@@ -66,18 +66,27 @@ def _plan(T, topo):
         oth = [c for c in m if not topo.may_write(c, mate)]
         if len(own) != len(oth):
             own, oth = m[0::2], m[1::2]
-        c_c, c_s, c_r, c_o = own[0], own[1], oth[0], oth[1]
+        c_x, c_s, c_y, c_o = own[0], own[1], oth[0], oth[1]
+        hq = nq // 2
         jobs[c_o] = [(mem[h][q], h) for q in range(nq)]
         jobs[c_s] = [(mem[sw[h]][q], h) for q in range(nq)]
-        jobs[c_c] = [(mem[cb[h]][q], h) for q in range(nq)]
-        jobs[c_r] = [(mem[cb[h]][q], sw[h]) if q in SWITCH_FIRST else (mem[sw[h]][q], cb[h]) for q in range(nq)]
+        jobs[c_x] = [(mem[cb[h]][q], h) for q in range(hq)] + [(mem[cb[h]][q], sw[h]) for q in range(hq)]
+        jobs[c_y] = [(mem[cb[h]][q], h) for q in range(hq, nq)] + [(mem[cb[h]][q], sw[h]) for q in range(hq, nq)]
+        groups[c_o] = groups[c_s] = [list(range(nq))]
+        groups[c_x] = groups[c_y] = [list(range(hq)), list(range(hq, nq))]
     handler = {}
     for c in cores:
         for k, (d, hs) in enumerate(jobs[c]):
             handler[(d, hs)] = (c, k)
 
-    plan = {c: {"jobs": jobs[c], "w_expect": 0, "x_expect": [0] * nq, "y_expect": [0] * len(hosts),
-                "self_w": None, "self_res": None} for c in cores}
+    plan = {}
+    for c in cores:
+        served = []
+        for d, hs in jobs[c]:
+            if d not in served:
+                served.append(d)
+        plan[c] = {"jobs": jobs[c], "groups": groups[c], "served": served, "w_expect": 0,
+                   "x_expect": [[0] * nq for gr in groups[c]], "y_expect": [0] * len(hosts), "self_res": None}
     for c in cores:
         p = plan[c]
         h = topo.host(c)
@@ -89,71 +98,65 @@ def _plan(T, topo):
         hi = [e for e in on if e not in off]
         half = len(off) // 2
 
-        wd = [handler[(c, hs)] for hs in hosts]
-        for rc, k in wd:
-            if rc == c:
-                p["self_w"] = k
-            else:
+        wd = []
+        for hs in hosts:
+            rc = handler[(c, hs)][0]
+            if rc != c and rc not in wd:
+                wd.append(rc)
                 plan[rc]["w_expect"] += len(off)
-        p["wsend"] = (_mk(off), [(rc, k) for rc, k in wd if rc != c])
+        p["wsend"] = (_mk(off), [(rc, plan[rc]["served"].index(c)) for rc in wd])
 
         msgs = []
-        for hd in hosts:
+        for hd in (dg[h], cb[h], sw[h], h):
             q = 0
             while q < nq:
                 rc, k = handler[(mem[hd][q], h)]
                 n = 1
                 while q + n < nq and handler[(mem[hd][q + n], h)] == (rc, k + n):
                     n += 1
-                msgs.append((rc, TK * rank[mem[hd][q]], TK * n, a * nq * TK + TK * k, hosts.index(hd)))
+                gr = [i for i, ks in enumerate(groups[rc]) if k in ks][0]
+                msgs.append((rc, TK * rank[mem[hd][q]], TK * n, a * nq * TK + TK * k, hosts.index(hd), gr))
                 q += n
         offm = [m for m in msgs if not same_chip(c, m[0])]
-        onm = [m for m in msgs if m[0] != c and same_chip(c, m[0])]
+        narrow = [m for m in msgs if m[0] != c and same_chip(c, m[0]) and m[2] == offm[0][2]]
+        wide = [m for m in msgs if m[0] != c and same_chip(c, m[0]) and m[2] != offm[0][2]]
         selfm = [m for m in msgs if m[0] == c]
-        if len(onm) <= 2:
-            on_sets, pool = [hi[:half], hi[half:]], off
-        else:
-            on_sets, pool = [hi[:half], hi[half:], off[half:]], (off[:half] if len(offm) == 1 else off)
-        per = len(pool) // len(offm)
-        sends = [(m, pool[i * per:(i + 1) * per]) for i, m in enumerate(offm)]
-        sends += [(m, on_sets[i]) for i, m in enumerate(onm)]
-        calls = []
-        for m, engines in sends:
-            plan[m[0]]["x_expect"][a] += len(engines)
-            hit = [cl for cl in calls if cl[0] == m[2]]
-            if not hit:
-                hit = [(m[2], [])]
-                calls.append(hit[0])
-            hit[0][1].append((m, _mk(engines)))
-        p["xcalls"] = [cl[1] for cl in calls]
+        per = len(off) // len(offm)
+        first = [(m, off[i * per:(i + 1) * per]) for i, m in enumerate(offm)]
+        first += [(m, (hi[:half], hi[half:])[i]) for i, m in enumerate(narrow)]
+        second = [(m, (hi, off)[i]) for i, m in enumerate(wide)]
+        p["xcalls"] = []
+        for call in (first, second):
+            for m, engines in call:
+                plan[m[0]]["x_expect"][m[5]][a] += len(engines)
+            p["xcalls"].append([(m, _mk(engines)) for m, engines in call])
         order = []
-        for m in offm + onm + selfm:
+        for m in offm + narrow + wide + selfm:
             if m[4] not in order:
                 order.append(m[4])
         p["loads"] = order
         p["slab_col"] = [TK * rank[mem[hd][0]] for hd in hosts]
         p["self_slabs"] = [m[4] for m in selfm]
+        p["a"] = a
 
-        rhs = []
-        for k, (d, hs) in enumerate(jobs[c]):
-            rhs.append([("xs", TK * rank[d]) if mem[hs][s] == c else ("xl", s * nq * TK + TK * k)
-                        for s in range(nq)])
-        p["rhs"] = rhs
-        p["a_order"] = ([a] if selfm else []) + [s for s in range(nq) if not (selfm and s == a)]
-        p["a_self"] = a if selfm else None
+        p["rhs"] = [[("xs", TK * rank[d]) if mem[hs][s] == c else ("xl", s * nq * TK + TK * k) for s in range(nq)]
+                    for k, (d, hs) in enumerate(jobs[c])]
 
-        outs = [(d, k, hosts.index(hs)) for k, (d, hs) in enumerate(jobs[c]) if d != c]
-        for k, (d, hs) in enumerate(jobs[c]):
-            if d == c:
-                p["self_res"] = (k, hosts.index(hs))
-        pool = on if all(same_chip(c, d) for d, k, s in outs) else off
-        per = 1
-        while per * 2 * len(outs) <= len(pool):
-            per *= 2
         p["rsend"] = []
-        for i, (d, k, s) in enumerate(outs):
-            p["rsend"].append((d, k, s, _mk(pool[i * per:(i + 1) * per])))
-            plan[d]["y_expect"][s] += per
+        for ks in groups[c]:
+            outs = [(jobs[c][k][0], k, hosts.index(jobs[c][k][1])) for k in ks if jobs[c][k][0] != c]
+            for k in ks:
+                if jobs[c][k][0] == c:
+                    p["self_res"] = (k, hosts.index(jobs[c][k][1]))
+            pool = on if all(same_chip(c, d) for d, k, s in outs) else off
+            per = 1
+            while per * 2 * len(outs) <= len(pool):
+                per *= 2
+            call = []
+            for i, (d, k, s) in enumerate(outs):
+                call.append((d, k, s, _mk(pool[i * per:(i + 1) * per])))
+                plan[d]["y_expect"][s] += per
+            p["rsend"].append(call)
         p["stores"] = [hosts.index(x) for x in (h, sw[h], cb[h], dg[h])]
     return plan
 
@@ -184,16 +187,15 @@ def rank_program(g, core, T, topo):
                        local_sem=S.sent)
     sent += len(_bits(mask))
 
-    a_me = None
     waited = []
     for call in p["xcalls"]:
         trs = []
-        for (d, c0, width, d0, s), mask in call:
+        for (d, c0, width, d0, s, gr), mask in call:
             if s not in waited:
                 g.wait_ge(S["ld%d" % s], 16)
                 waited.append(s)
-            a_me = d0 // slab
-            trs.append(RemoteDMATransfer(dst_ids=[dst_id(d)], dma_engine_mask=mask, remote_sem=S["x%d" % a_me],
+            trs.append(RemoteDMATransfer(dst_ids=[dst_id(d)], dma_engine_mask=mask,
+                                         remote_sem=S["x%d_%d" % (gr, p["a"])],
                                          src=T.xs[:, c0:c0 + width], dst=T.xl[:, d0:d0 + width]))
             sent += len(_bits(mask))
         g.remote_dma_fused(trs, local_sem=S.sent)
@@ -202,45 +204,49 @@ def rank_program(g, core, T, topo):
     v.memset(T.z[:], 0.0).then_inc(S.ms, 1)
     v.wait_ge(S.ms, 1)
     v.wait_ge(S.w, p["w_expect"])
-    if p["self_w"] is not None:
+    if core in p["served"]:
         v.wait_ge(S.ldw, 16)
-    for k in range(nq):
-        src = T.ws[:] if k == p["self_w"] else T.wl[:, F * k:F * k + F]
-        v.tensor_copy(T.z[:, ZP * k + 3:ZP * k + 3 + 4 * F:4], src).then_inc(S.z, 1)
+    for i, d in enumerate(p["served"]):
+        src = T.ws[:] if d == core else T.wl[:, F * i:F * i + F]
+        v.tensor_copy(T.z[:, ZP * i + 3:ZP * i + 3 + 4 * F:4], src).then_inc(S.z, 1)
 
     t = g.tensor
-    t.wait_ge(S.z, nq)
-    order = p["a_order"]
-    for i, a in enumerate(order):
-        if a == p["a_self"]:
-            for s in p["self_slabs"]:
-                t.wait_ge(S["ld%d" % s], 16)
-        else:
-            t.wait_ge(S["x%d" % a], p["x_expect"][a])
-        for k in range(nq):
-            name, c0 = p["rhs"][k][a]
-            mm = t.matmul(T["p%d" % k][:, 0:TK], T.z[:, ZP * k + 3 - a:ZP * k + 3 - a + 128], T[name][:, c0:c0 + TK],
-                          i == 0, i == len(order) - 1)
-            if i == len(order) - 1:
-                mm.then_inc(S["mm%d" % k], 1)
+    t.wait_ge(S.z, len(p["served"]))
+    for gi, ks in enumerate(p["groups"]):
+        own = p["rhs"][ks[0]][p["a"]][0] == "xs"
+        order = ([p["a"]] if own else []) + [s for s in range(nq) if not (own and s == p["a"])]
+        for i, a in enumerate(order):
+            if own and a == p["a"]:
+                for s in p["self_slabs"]:
+                    t.wait_ge(S["ld%d" % s], 16)
+            else:
+                t.wait_ge(S["x%d_%d" % (gi, a)], p["x_expect"][gi][a])
+            for k in ks:
+                name, c0 = p["rhs"][k][a]
+                z0 = ZP * p["served"].index(p["jobs"][k][0]) + 3 - a
+                mm = t.matmul(T["p%d" % k][:, 0:TK], T.z[:, z0:z0 + 128], T[name][:, c0:c0 + TK],
+                              i == 0, i == len(order) - 1)
+                if i == len(order) - 1:
+                    mm.then_inc(S["mm%d" % k], 1)
 
-    for k in range(nq):
-        v.wait_ge(S["mm%d" % k], 1)
-        v.tensor_copy(T.res[:, TK * k:TK * k + TK], T["p%d" % k][:, 0:TK]).then_inc(S.cp, 1)
-    g.wait_ge(S.cp, nq)
-    trs = []
-    for d, k, s, mask in p["rsend"]:
-        trs.append(RemoteDMATransfer(dst_ids=[dst_id(d)], dma_engine_mask=mask, remote_sem=S["y%d" % s],
-                                     src=T.res[:, TK * k:TK * k + TK], dst=T.yl[s]))
-        sent += len(_bits(mask))
-    g.remote_dma_fused(trs, local_sem=S.sent)
+    for gi, ks in enumerate(p["groups"]):
+        for k in ks:
+            v.wait_ge(S["mm%d" % k], 1)
+            v.tensor_copy(T.res[:, TK * k:TK * k + TK], T["p%d" % k][:, 0:TK]).then_inc(S["cp%d" % gi], 1)
+        g.wait_ge(S["cp%d" % gi], len(ks))
+        trs = []
+        for d, k, s, mask in p["rsend"][gi]:
+            trs.append(RemoteDMATransfer(dst_ids=[dst_id(d)], dma_engine_mask=mask, remote_sem=S["y%d" % s],
+                                         src=T.res[:, TK * k:TK * k + TK], dst=T.yl[s]))
+            sent += len(_bits(mask))
+        g.remote_dma_fused(trs, local_sem=S.sent)
 
     for i, s in enumerate(p["stores"]):
         q = g.sync if i in (0, 3) else g.scalar
         c0 = p["slab_col"][s]
         if p["self_res"] is not None and p["self_res"][1] == s:
             k = p["self_res"][0]
-            q.wait_ge(S.cp, nq)
+            q.wait_ge(S.cp0, nq)
             q.dma_start(T.y[:, c0:c0 + slab], T.res[:, TK * k:TK * k + TK]).then_inc(S.st, 16)
         else:
             q.wait_ge(S["y%d" % s], p["y_expect"][s])

@@ -14,11 +14,12 @@ SCRATCH = {
     "p1": ("psum", [128, 512], "float32"),
     "p2": ("psum", [128, 512], "float32"),
     "p3": ("psum", [128, 512], "float32"),
+    "fl": ("dram", [1, 128, TK], "bfloat16"),
     "yl": ("dram", [4, 128, TK], "bfloat16"),
 }
-SEMAPHORES = ["ldw", "ld0", "ld1", "ld2", "ld3", "ms", "w", "z", "x0_0", "x0_1", "x0_2", "x0_3",
-              "x1_0", "x1_1", "x1_2", "x1_3", "mm0", "mm1", "mm2", "mm3", "cp0", "cp1",
-              "y0", "y1", "y2", "y3", "st", "sent"]
+SEMAPHORES = ["ldw", "ld0", "ld1", "ld2", "ld3", "ms", "wa", "wb", "z0", "z1", "z2",
+              "x0_0", "x0_1", "x0_2", "x0_3", "x1_0", "x1_1", "x1_2", "x1_3", "x2_0", "x2_1", "x2_2", "x2_3",
+              "mm0", "mm1", "mm2", "mm3", "cp0", "cp1", "cp2", "f", "y0", "y1", "y2", "y3", "st", "sent"]
 
 
 def _bits(mask):
@@ -32,6 +33,13 @@ def _mk(engines):
     return m
 
 
+def _share(pool, n):
+    per = 1
+    while per * 2 * n <= len(pool):
+        per *= 2
+    return per
+
+
 def _plan(T, topo):
     cores = list(T.cores)
     rank = {c: i for i, c in enumerate(cores)}
@@ -41,6 +49,7 @@ def _plan(T, topo):
             hosts.append(topo.host(c))
     mem = {h: [c for c in cores if topo.host(c) == h] for h in hosts}
     nq = len(mem[hosts[0]])
+    hq = nq // 2
     sw, cb, dg = {}, {}, {}
     for h in hosts:
         for k in hosts:
@@ -57,7 +66,9 @@ def _plan(T, topo):
     def same_chip(a, b):
         return topo.host(a) == topo.host(b) and topo.chip(a) == topo.chip(b)
 
-    jobs, groups = {}, {}
+    jobs, roles, ridx, cside, helpers = {}, {}, {}, {}, {}
+    groups = [list(range(hq)), [hq], [hq + 1]]
+    halves = [list(range(hq)), list(range(hq, nq))]
     for h in hosts:
         m = mem[h]
         base = m[0] - m[0] % topo.CORES_PER_HOST
@@ -66,27 +77,28 @@ def _plan(T, topo):
         oth = [c for c in m if not topo.may_write(c, mate)]
         if len(own) != len(oth):
             own, oth = m[0::2], m[1::2]
-        c_x, c_s, c_y, c_o = own[0], own[1], oth[0], oth[1]
-        hq = nq // 2
-        jobs[c_o] = [(mem[h][q], h) for q in range(nq)]
-        jobs[c_s] = [(mem[sw[h]][q], h) for q in range(nq)]
-        jobs[c_x] = [(mem[cb[h]][q], h) for q in range(hq)] + [(mem[cb[h]][q], sw[h]) for q in range(hq)]
-        jobs[c_y] = [(mem[cb[h]][q], h) for q in range(hq, nq)] + [(mem[cb[h]][q], sw[h]) for q in range(hq, nq)]
-        groups[c_o] = groups[c_s] = [list(range(nq))]
-        groups[c_x] = groups[c_y] = [list(range(hq)), list(range(hq, nq))]
+        roles[h] = [own[0], oth[0], own[1], oth[1]]
+        for i, (c, nb, hf) in enumerate(zip(roles[h], (cb[h], cb[h], sw[h], sw[h]), (0, 1, 0, 1))):
+            jobs[c] = [(mem[nb][q], h) for q in halves[hf]] + [(c, h), (mem[dg[h]][m.index(c)], h)]
+            ridx[c] = i
+            cside[c] = nb == cb[h]
+        helpers[h] = [x for x in range(base, base + topo.CORES_PER_HOST)
+                      if same_chip(x, m[0]) and topo.die(x) != topo.die(m[0])]
     handler = {}
     for c in cores:
         for k, (d, hs) in enumerate(jobs[c]):
             handler[(d, hs)] = (c, k)
 
+    def grp(k):
+        return [i for i, ks in enumerate(groups) if k in ks][0]
+
     plan = {}
     for c in cores:
-        served = []
-        for d, hs in jobs[c]:
-            if d not in served:
-                served.append(d)
-        plan[c] = {"jobs": jobs[c], "groups": groups[c], "served": served, "w_expect": 0,
-                   "x_expect": [[0] * nq for gr in groups[c]], "y_expect": [0] * len(hosts), "self_res": None}
+        plan[c] = {"jobs": jobs[c], "groups": groups, "wa": 0, "wb": 0, "wfwd": None, "fwd": [], "f_expect": 0,
+                   "x_expect": [[0] * nq for gr in groups], "y_expect": [0] * len(hosts), "self_res": None}
+    for h in hosts:
+        for x in helpers[h]:
+            plan[x] = {"helper": True, "fwd": [], "f_expect": 0}
     for c in cores:
         p = plan[c]
         h = topo.host(c)
@@ -95,83 +107,115 @@ def _plan(T, topo):
         near = [d for d in cores if d != c and same_chip(c, d)][0]
         off = _bits(topo.mask(c, far))
         on = _bits(topo.mask(c, near))
-        hi = [e for e in on if e not in off]
+        top = on[::-1]
         half = len(off) // 2
 
-        wd = []
-        for hs in hosts:
-            rc = handler[(c, hs)][0]
-            if rc != c and rc not in wd:
-                wd.append(rc)
-                plan[rc]["w_expect"] += len(off)
-        p["wsend"] = (_mk(off), [(rc, plan[rc]["served"].index(c)) for rc in wd])
+        hc, hs_ = handler[(c, cb[h])], handler[(c, sw[h])]
+        p["wsend"] = [(_mk(off[:half]), hc), (_mk(off[half:]), hs_)]
+        plan[hc[0]]["wa"] += half
+        plan[hs_[0]]["wa"] += half
+        fw = hc if hc[1] == groups[0][0] else hs_
+        tc, tk = handler[(c, dg[h])]
+        assert plan[fw[0]]["wfwd"] is None and topo.may_write(fw[0], tc)
+        plan[fw[0]]["wfwd"] = (tc, fw[1], tk, topo.mask(fw[0], tc))
+        plan[tc]["wb"] += len(_bits(topo.mask(fw[0], tc)))
 
-        msgs = []
-        for hd in (dg[h], cb[h], sw[h], h):
-            q = 0
-            while q < nq:
-                rc, k = handler[(mem[hd][q], h)]
-                n = 1
-                while q + n < nq and handler[(mem[hd][q + n], h)] == (rc, k + n):
-                    n += 1
-                gr = [i for i, ks in enumerate(groups[rc]) if k in ks][0]
-                msgs.append((rc, TK * rank[mem[hd][q]], TK * n, a * nq * TK + TK * k, hosts.index(hd), gr))
-                q += n
-        offm = [m for m in msgs if not same_chip(c, m[0])]
-        narrow = [m for m in msgs if m[0] != c and same_chip(c, m[0]) and m[2] == offm[0][2]]
-        wide = [m for m in msgs if m[0] != c and same_chip(c, m[0]) and m[2] != offm[0][2]]
-        selfm = [m for m in msgs if m[0] == c]
-        per = len(off) // len(offm)
-        first = [(m, off[i * per:(i + 1) * per]) for i, m in enumerate(offm)]
-        first += [(m, (hi[:half], hi[half:])[i]) for i, m in enumerate(narrow)]
-        second = [(m, (hi, off)[i]) for i, m in enumerate(wide)]
-        p["xcalls"] = []
-        for call in (first, second):
-            for m, engines in call:
-                plan[m[0]]["x_expect"][m[5]][a] += len(engines)
-            p["xcalls"].append([(m, _mk(engines)) for m, engines in call])
-        order = []
-        for m in offm + narrow + wide + selfm:
-            if m[4] not in order:
-                order.append(m[4])
-        p["loads"] = order
+        calls = []
+        for pair in ((cb[h], sw[h]), (h, dg[h])):
+            msgs = []
+            for hd in pair:
+                q = 0
+                while q < nq:
+                    rc, k = handler[(mem[hd][q], h)]
+                    n = 1
+                    while q + n < nq and handler[(mem[hd][q + n], h)] == (rc, k + n):
+                        n += 1
+                    if rc != c:
+                        msgs.append((rc, TK * rank[mem[hd][q]], TK * n, a * nq * TK + TK * k, hosts.index(hd), grp(k)))
+                    q += n
+            per = _share(top, len(msgs))
+            call = []
+            for i, m in enumerate(msgs):
+                call.append((m, _mk(top[i * per:(i + 1) * per])))
+                plan[m[0]]["x_expect"][m[5]][a] += per
+            calls.append(call)
+        p["xcalls"] = calls
+        p["loads"] = [hosts.index(hd) for hd in (cb[h], sw[h], h, dg[h])]
         p["slab_col"] = [TK * rank[mem[hd][0]] for hd in hosts]
-        p["self_slabs"] = [m[4] for m in selfm]
+        p["gslab"] = [hosts.index(topo.host(jobs[c][ks[0]][0])) for ks in groups]
         p["a"] = a
 
-        p["rhs"] = [[("xs", TK * rank[d]) if mem[hs][s] == c else ("xl", s * nq * TK + TK * k) for s in range(nq)]
+        p["rhs"] = [[("xs", TK * rank[d]) if mem[h][s] == c else ("xl", s * nq * TK + TK * k) for s in range(nq)]
                     for k, (d, hs) in enumerate(jobs[c])]
 
         p["rsend"] = []
-        for ks in groups[c]:
-            outs = [(jobs[c][k][0], k, hosts.index(jobs[c][k][1])) for k in ks if jobs[c][k][0] != c]
-            for k in ks:
-                if jobs[c][k][0] == c:
-                    p["self_res"] = (k, hosts.index(jobs[c][k][1]))
-            pool = on if all(same_chip(c, d) for d, k, s in outs) else off
-            per = 1
-            while per * 2 * len(outs) <= len(pool):
-                per *= 2
+        s = hosts.index(h)
+        for gi, ks in enumerate(groups):
+            outs = []
+            for i, k in enumerate(ks):
+                d = jobs[c][k][0]
+                if d == c:
+                    p["self_res"] = (k, s, gi)
+                    continue
+                if not topo.may_write(c, d):
+                    via = roles[cb[h] if cside[c] else sw[h]][ridx[c]]
+                elif topo.host(d) == cb[h]:
+                    via = helpers[h][(len(ks) * ridx[c] + i) % len(helpers[h])]
+                else:
+                    via = None
+                if via is None:
+                    outs.append((d, k, "yl", s, "y%d" % s))
+                else:
+                    outs.append((via, k, "fl", 0, "f"))
+                    assert not plan[via]["fwd"]
+                    plan[via]["fwd"].append((d, s, topo.mask(via, d)))
+                    plan[d]["y_expect"][s] += len(_bits(topo.mask(via, d)))
+            pool = on if all(same_chip(c, o[0]) for o in outs) else off
+            per = _share(pool, len(outs)) if outs else 0
             call = []
-            for i, (d, k, s) in enumerate(outs):
-                call.append((d, k, s, _mk(pool[i * per:(i + 1) * per])))
-                plan[d]["y_expect"][s] += per
+            for i, o in enumerate(outs):
+                call.append(o + (_mk(pool[i * per:(i + 1) * per]),))
+                if o[2] == "yl":
+                    plan[o[0]]["y_expect"][s] += per
+                else:
+                    plan[o[0]]["f_expect"] += per
             p["rsend"].append(call)
         p["stores"] = [hosts.index(x) for x in (h, sw[h], cb[h], dg[h])]
     return plan
 
 
 def rank_program(g, core, T, topo):
-    if T.rank_of(core) is None:
+    if not [c for c in T.cores if topo.host(c) == topo.host(core) and topo.chip(c) == topo.chip(core)]:
         return
-    p = _plan(T, topo)[core]
+    plan = _plan(T, topo)
+    if core not in plan:
+        return
+    p = plan[core]
     S = T.sem
-    nq = len(p["jobs"])
-    slab = nq * TK
+    sent = [0]
 
     def dst_id(d):
         rid, pid = topo.addr(d, core)
         return DstId(rid=rid, pnc=pid)
+
+    def fused(trs, masks):
+        g.remote_dma_fused(trs, local_sem=S.sent)
+        for m in masks:
+            sent[0] += len(_bits(m))
+
+    def pass_on():
+        g.wait_ge(S.f, p["f_expect"])
+        fused([RemoteDMATransfer(dst_ids=[dst_id(d)], dma_engine_mask=mask, remote_sem=S["y%d" % s],
+                                 src=T.fl[0], dst=T.yl[s]) for d, s, mask in p["fwd"]], [o[2] for o in p["fwd"]])
+
+    if "helper" in p:
+        if p["fwd"]:
+            pass_on()
+            g.wait_ge(S.sent, sent[0])
+        return
+
+    nq = len(p["jobs"])
+    slab = nq * TK
 
     g.sync.dma_start(T.ws[:], T.w[:]).then_inc(S.ldw, 16)
     for i, s in enumerate(p["loads"]):
@@ -179,16 +223,13 @@ def rank_program(g, core, T, topo):
         c0 = p["slab_col"][s]
         q.dma_start(T.xs[:, c0:c0 + slab], T.x[:, c0:c0 + slab]).then_inc(S["ld%d" % s], 16)
 
-    sent = 0
-    mask, dests = p["wsend"]
     g.wait_ge(S.ldw, 16)
-    g.remote_dma_fused([RemoteDMATransfer(dst_ids=[dst_id(d) for d, k in dests], dma_engine_mask=mask, remote_sem=S.w,
-                                          srcs=[T.ws[:]], dsts=[T.wl[:, F * k:F * k + F] for d, k in dests])],
-                       local_sem=S.sent)
-    sent += len(_bits(mask))
+    fused([RemoteDMATransfer(dst_ids=[dst_id(d)], dma_engine_mask=mask, remote_sem=S.wa,
+                             src=T.ws[:], dst=T.wl[:, F * k:F * k + F]) for mask, (d, k) in p["wsend"]],
+          [mask for mask, dk in p["wsend"]])
 
-    waited = []
     for call in p["xcalls"]:
+        waited = []
         trs = []
         for (d, c0, width, d0, s, gr), mask in call:
             if s not in waited:
@@ -197,60 +238,69 @@ def rank_program(g, core, T, topo):
             trs.append(RemoteDMATransfer(dst_ids=[dst_id(d)], dma_engine_mask=mask,
                                          remote_sem=S["x%d_%d" % (gr, p["a"])],
                                          src=T.xs[:, c0:c0 + width], dst=T.xl[:, d0:d0 + width]))
-            sent += len(_bits(mask))
-        g.remote_dma_fused(trs, local_sem=S.sent)
+        fused(trs, [mask for m, mask in call])
+
+    d, k0, k1, mask = p["wfwd"]
+    g.wait_ge(S.wa, p["wa"])
+    fused([RemoteDMATransfer(dst_ids=[dst_id(d)], dma_engine_mask=mask, remote_sem=S.wb,
+                             src=T.wl[:, F * k0:F * k0 + F], dst=T.wl[:, F * k1:F * k1 + F])], [mask])
 
     v = g.vector
     v.memset(T.z[:], 0.0).then_inc(S.ms, 1)
     v.wait_ge(S.ms, 1)
-    v.wait_ge(S.w, p["w_expect"])
-    if core in p["served"]:
-        v.wait_ge(S.ldw, 16)
-    for i, d in enumerate(p["served"]):
-        src = T.ws[:] if d == core else T.wl[:, F * i:F * i + F]
-        v.tensor_copy(T.z[:, ZP * i + 3:ZP * i + 3 + 4 * F:4], src).then_inc(S.z, 1)
+
+    def spread(gi):
+        for sem, n in ((S.wa, p["wa"]), (S.ldw, 16), (S.wb, p["wb"]))[gi:gi + 1]:
+            v.wait_ge(sem, n)
+        for k in p["groups"][gi]:
+            src = T.ws[:] if p["jobs"][k][0] == core else T.wl[:, F * k:F * k + F]
+            v.tensor_copy(T.z[:, ZP * k + 3:ZP * k + 3 + 4 * F:4], src).then_inc(S["z%d" % gi], 1)
+
+    def round_off(gi):
+        for k in p["groups"][gi]:
+            v.wait_ge(S["mm%d" % k], 1)
+            v.tensor_copy(T.res[:, TK * k:TK * k + TK], T["p%d" % k][:, 0:TK]).then_inc(S["cp%d" % gi], 1)
+
+    for step, gi in ((spread, 1), (spread, 0), (round_off, 0), (round_off, 1), (spread, 2), (round_off, 2)):
+        step(gi)
 
     t = g.tensor
-    t.wait_ge(S.z, len(p["served"]))
     for gi, ks in enumerate(p["groups"]):
-        own = p["rhs"][ks[0]][p["a"]][0] == "xs"
-        order = ([p["a"]] if own else []) + [s for s in range(nq) if not (own and s == p["a"])]
+        t.wait_ge(S["z%d" % gi], len(ks))
+        order = [p["a"]] + [s for s in range(nq) if s != p["a"]]
         for i, a in enumerate(order):
-            if own and a == p["a"]:
-                for s in p["self_slabs"]:
-                    t.wait_ge(S["ld%d" % s], 16)
+            if a == p["a"]:
+                t.wait_ge(S["ld%d" % p["gslab"][gi]], 16)
             else:
                 t.wait_ge(S["x%d_%d" % (gi, a)], p["x_expect"][gi][a])
             for k in ks:
                 name, c0 = p["rhs"][k][a]
-                z0 = ZP * p["served"].index(p["jobs"][k][0]) + 3 - a
+                z0 = ZP * k + 3 - a
                 mm = t.matmul(T["p%d" % k][:, 0:TK], T.z[:, z0:z0 + 128], T[name][:, c0:c0 + TK],
                               i == 0, i == len(order) - 1)
                 if i == len(order) - 1:
                     mm.then_inc(S["mm%d" % k], 1)
 
     for gi, ks in enumerate(p["groups"]):
-        for k in ks:
-            v.wait_ge(S["mm%d" % k], 1)
-            v.tensor_copy(T.res[:, TK * k:TK * k + TK], T["p%d" % k][:, 0:TK]).then_inc(S["cp%d" % gi], 1)
+        if not p["rsend"][gi]:
+            continue
         g.wait_ge(S["cp%d" % gi], len(ks))
-        trs = []
-        for d, k, s, mask in p["rsend"][gi]:
-            trs.append(RemoteDMATransfer(dst_ids=[dst_id(d)], dma_engine_mask=mask, remote_sem=S["y%d" % s],
-                                         src=T.res[:, TK * k:TK * k + TK], dst=T.yl[s]))
-            sent += len(_bits(mask))
-        g.remote_dma_fused(trs, local_sem=S.sent)
+        fused([RemoteDMATransfer(dst_ids=[dst_id(d)], dma_engine_mask=mask, remote_sem=S[sem],
+                                 src=T.res[:, TK * k:TK * k + TK], dst=T[buf][slot])
+               for d, k, buf, slot, sem, mask in p["rsend"][gi]], [o[5] for o in p["rsend"][gi]])
+
+    pass_on()
 
     for i, s in enumerate(p["stores"]):
         q = g.sync if i in (0, 3) else g.scalar
         c0 = p["slab_col"][s]
         if p["self_res"] is not None and p["self_res"][1] == s:
-            k = p["self_res"][0]
-            q.wait_ge(S.cp0, nq)
+            k, s_, gi = p["self_res"]
+            q.wait_ge(S["cp%d" % gi], len(p["groups"][gi]))
             q.dma_start(T.y[:, c0:c0 + slab], T.res[:, TK * k:TK * k + TK]).then_inc(S.st, 16)
         else:
             q.wait_ge(S["y%d" % s], p["y_expect"][s])
             q.dma_start(T.y[:, c0:c0 + slab], T.yl[s]).then_inc(S.st, 16)
 
-    g.wait_ge(S.sent, sent)
+    g.wait_ge(S.sent, sent[0])
     g.wait_ge(S.st, 16 * len(p["stores"]))

from concourse.bass import DstId, RemoteDMATransfer

TK, F = 128, 32
ZP = 136

SCRATCH = {
    "xs": ("sbuf", [128, 16 * TK], "bfloat16"),
    "ws": ("sbuf", [128, F], "bfloat16"),
    "wl": ("sbuf", [128, 4 * F], "bfloat16"),
    "z": ("sbuf", [128, 4 * ZP], "bfloat16"),
    "xl": ("sbuf", [128, 16 * TK], "bfloat16"),
    "res": ("sbuf", [128, 4 * TK], "bfloat16"),
    "p0": ("psum", [128, 512], "float32"),
    "p1": ("psum", [128, 512], "float32"),
    "p2": ("psum", [128, 512], "float32"),
    "p3": ("psum", [128, 512], "float32"),
    "fl": ("dram", [1, 128, TK], "bfloat16"),
    "yl": ("dram", [4, 128, TK], "bfloat16"),
}
SEMAPHORES = ["ldw", "ld0", "ld1", "ld2", "ld3", "ms", "wa", "wb", "z0", "z1", "z2",
              "x0_0", "x0_1", "x0_2", "x0_3", "x1_0", "x1_1", "x1_2", "x1_3", "x2_0", "x2_1", "x2_2", "x2_3",
              "mm0", "mm1", "mm2", "mm3", "cp0", "cp1", "cp2", "f", "y0", "y1", "y2", "y3", "st", "sent"]


def _bits(mask):
    return [e for e in range(mask.bit_length()) if (mask >> e) & 1]


def _mk(engines):
    m = 0
    for e in engines:
        m |= 1 << e
    return m


def _share(pool, n):
    per = 1
    while per * 2 * n <= len(pool):
        per *= 2
    return per


def _plan(T, topo):
    cores = list(T.cores)
    rank = {c: i for i, c in enumerate(cores)}
    hosts = []
    for c in cores:
        if topo.host(c) not in hosts:
            hosts.append(topo.host(c))
    mem = {h: [c for c in cores if topo.host(c) == h] for h in hosts}
    nq = len(mem[hosts[0]])
    hq = nq // 2
    sw, cb, dg = {}, {}, {}
    for h in hosts:
        for k in hosts:
            if k == h:
                continue
            a, b = mem[h][0], mem[k][0]
            if not topo.may_write(a, b):
                dg[h] = k
            elif topo.same_plane(a, b):
                sw[h] = k
            else:
                cb[h] = k

    def same_chip(a, b):
        return topo.host(a) == topo.host(b) and topo.chip(a) == topo.chip(b)

    jobs, roles, ridx, cside, helpers = {}, {}, {}, {}, {}
    groups = [list(range(hq)), [hq], [hq + 1]]
    halves = [list(range(hq)), list(range(hq, nq))]
    for h in hosts:
        m = mem[h]
        base = m[0] - m[0] % topo.CORES_PER_HOST
        mate = [x for x in range(base, base + topo.CORES_PER_HOST) if topo.mates(m[0], x)][0]
        own = [c for c in m if topo.may_write(c, mate)]
        oth = [c for c in m if not topo.may_write(c, mate)]
        if len(own) != len(oth):
            own, oth = m[0::2], m[1::2]
        roles[h] = [own[0], oth[0], own[1], oth[1]]
        for i, (c, nb, hf) in enumerate(zip(roles[h], (cb[h], cb[h], sw[h], sw[h]), (0, 1, 0, 1))):
            jobs[c] = [(mem[nb][q], h) for q in halves[hf]] + [(c, h), (mem[dg[h]][m.index(c)], h)]
            ridx[c] = i
            cside[c] = nb == cb[h]
        helpers[h] = [x for x in range(base, base + topo.CORES_PER_HOST)
                      if same_chip(x, m[0]) and topo.die(x) != topo.die(m[0])]
    handler = {}
    for c in cores:
        for k, (d, hs) in enumerate(jobs[c]):
            handler[(d, hs)] = (c, k)

    def grp(k):
        return [i for i, ks in enumerate(groups) if k in ks][0]

    plan = {}
    for c in cores:
        plan[c] = {"jobs": jobs[c], "groups": groups, "wa": 0, "wb": 0, "wfwd": None, "fwd": [], "f_expect": 0,
                   "x_expect": [[0] * nq for gr in groups], "y_expect": [0] * len(hosts), "self_res": None}
    for h in hosts:
        for x in helpers[h]:
            plan[x] = {"helper": True, "fwd": [], "f_expect": 0}
    for c in cores:
        p = plan[c]
        h = topo.host(c)
        a = mem[h].index(c)
        far = [d for d in cores if not same_chip(c, d) and topo.may_write(c, d)][0]
        near = [d for d in cores if d != c and same_chip(c, d)][0]
        off = _bits(topo.mask(c, far))
        on = _bits(topo.mask(c, near))
        top = on[::-1]
        half = len(off) // 2

        hc, hs_ = handler[(c, cb[h])], handler[(c, sw[h])]
        p["wsend"] = [(_mk(off[:half]), hc), (_mk(off[half:]), hs_)]
        plan[hc[0]]["wa"] += half
        plan[hs_[0]]["wa"] += half
        fw = hc if hc[1] == groups[0][0] else hs_
        tc, tk = handler[(c, dg[h])]
        assert plan[fw[0]]["wfwd"] is None and topo.may_write(fw[0], tc)
        plan[fw[0]]["wfwd"] = (tc, fw[1], tk, topo.mask(fw[0], tc))
        plan[tc]["wb"] += len(_bits(topo.mask(fw[0], tc)))

        calls = []
        for pair in ((cb[h], sw[h]), (h, dg[h])):
            msgs = []
            for hd in pair:
                q = 0
                while q < nq:
                    rc, k = handler[(mem[hd][q], h)]
                    n = 1
                    while q + n < nq and handler[(mem[hd][q + n], h)] == (rc, k + n):
                        n += 1
                    if rc != c:
                        msgs.append((rc, TK * rank[mem[hd][q]], TK * n, a * nq * TK + TK * k, hosts.index(hd), grp(k)))
                    q += n
            per = _share(top, len(msgs))
            call = []
            for i, m in enumerate(msgs):
                call.append((m, _mk(top[i * per:(i + 1) * per])))
                plan[m[0]]["x_expect"][m[5]][a] += per
            calls.append(call)
        p["xcalls"] = calls
        p["loads"] = [hosts.index(hd) for hd in (cb[h], sw[h], h, dg[h])]
        p["slab_col"] = [TK * rank[mem[hd][0]] for hd in hosts]
        p["gslab"] = [hosts.index(topo.host(jobs[c][ks[0]][0])) for ks in groups]
        p["a"] = a

        p["rhs"] = [[("xs", TK * rank[d]) if mem[h][s] == c else ("xl", s * nq * TK + TK * k) for s in range(nq)]
                    for k, (d, hs) in enumerate(jobs[c])]

        p["rsend"] = []
        s = hosts.index(h)
        for gi, ks in enumerate(groups):
            outs = []
            for i, k in enumerate(ks):
                d = jobs[c][k][0]
                if d == c:
                    p["self_res"] = (k, s, gi)
                    continue
                if not topo.may_write(c, d):
                    via = roles[cb[h] if cside[c] else sw[h]][ridx[c]]
                elif topo.host(d) == cb[h]:
                    via = helpers[h][(len(ks) * ridx[c] + i) % len(helpers[h])]
                else:
                    via = None
                if via is None:
                    outs.append((d, k, "yl", s, "y%d" % s))
                else:
                    outs.append((via, k, "fl", 0, "f"))
                    assert not plan[via]["fwd"]
                    plan[via]["fwd"].append((d, s, topo.mask(via, d)))
                    plan[d]["y_expect"][s] += len(_bits(topo.mask(via, d)))
            pool = on if all(same_chip(c, o[0]) for o in outs) else off
            per = _share(pool, len(outs)) if outs else 0
            call = []
            for i, o in enumerate(outs):
                call.append(o + (_mk(pool[i * per:(i + 1) * per]),))
                if o[2] == "yl":
                    plan[o[0]]["y_expect"][s] += per
                else:
                    plan[o[0]]["f_expect"] += per
            p["rsend"].append(call)
        p["stores"] = [hosts.index(x) for x in (h, sw[h], cb[h], dg[h])]
    return plan


def rank_program(g, core, T, topo):
    if not [c for c in T.cores if topo.host(c) == topo.host(core) and topo.chip(c) == topo.chip(core)]:
        return
    plan = _plan(T, topo)
    if core not in plan:
        return
    p = plan[core]
    S = T.sem
    sent = [0]

    def dst_id(d):
        rid, pid = topo.addr(d, core)
        return DstId(rid=rid, pnc=pid)

    def fused(trs, masks):
        g.remote_dma_fused(trs, local_sem=S.sent)
        for m in masks:
            sent[0] += len(_bits(m))

    def pass_on():
        g.wait_ge(S.f, p["f_expect"])
        fused([RemoteDMATransfer(dst_ids=[dst_id(d)], dma_engine_mask=mask, remote_sem=S["y%d" % s],
                                 src=T.fl[0], dst=T.yl[s]) for d, s, mask in p["fwd"]], [o[2] for o in p["fwd"]])

    if "helper" in p:
        if p["fwd"]:
            pass_on()
            g.wait_ge(S.sent, sent[0])
        return

    nq = len(p["jobs"])
    slab = nq * TK

    g.sync.dma_start(T.ws[:], T.w[:]).then_inc(S.ldw, 16)
    for i, s in enumerate(p["loads"]):
        q = g.scalar if i % 2 == 0 else g.sync
        c0 = p["slab_col"][s]
        q.dma_start(T.xs[:, c0:c0 + slab], T.x[:, c0:c0 + slab]).then_inc(S["ld%d" % s], 16)

    g.wait_ge(S.ldw, 16)
    fused([RemoteDMATransfer(dst_ids=[dst_id(d)], dma_engine_mask=mask, remote_sem=S.wa,
                             src=T.ws[:], dst=T.wl[:, F * k:F * k + F]) for mask, (d, k) in p["wsend"]],
          [mask for mask, dk in p["wsend"]])

    for call in p["xcalls"]:
        waited = []
        trs = []
        for (d, c0, width, d0, s, gr), mask in call:
            if s not in waited:
                g.wait_ge(S["ld%d" % s], 16)
                waited.append(s)
            trs.append(RemoteDMATransfer(dst_ids=[dst_id(d)], dma_engine_mask=mask,
                                         remote_sem=S["x%d_%d" % (gr, p["a"])],
                                         src=T.xs[:, c0:c0 + width], dst=T.xl[:, d0:d0 + width]))
        fused(trs, [mask for m, mask in call])

    d, k0, k1, mask = p["wfwd"]
    g.wait_ge(S.wa, p["wa"])
    fused([RemoteDMATransfer(dst_ids=[dst_id(d)], dma_engine_mask=mask, remote_sem=S.wb,
                             src=T.wl[:, F * k0:F * k0 + F], dst=T.wl[:, F * k1:F * k1 + F])], [mask])

    v = g.vector
    v.memset(T.z[:], 0.0).then_inc(S.ms, 1)
    v.wait_ge(S.ms, 1)

    def spread(gi):
        for sem, n in ((S.wa, p["wa"]), (S.ldw, 16), (S.wb, p["wb"]))[gi:gi + 1]:
            v.wait_ge(sem, n)
        for k in p["groups"][gi]:
            src = T.ws[:] if p["jobs"][k][0] == core else T.wl[:, F * k:F * k + F]
            v.tensor_copy(T.z[:, ZP * k + 3:ZP * k + 3 + 4 * F:4], src).then_inc(S["z%d" % gi], 1)

    def round_off(gi):
        for k in p["groups"][gi]:
            v.wait_ge(S["mm%d" % k], 1)
            v.tensor_copy(T.res[:, TK * k:TK * k + TK], T["p%d" % k][:, 0:TK]).then_inc(S["cp%d" % gi], 1)

    for step, gi in ((spread, 1), (spread, 0), (round_off, 0), (round_off, 1), (spread, 2), (round_off, 2)):
        step(gi)

    t = g.tensor
    for gi, ks in enumerate(p["groups"]):
        t.wait_ge(S["z%d" % gi], len(ks))
        order = [p["a"]] + [s for s in range(nq) if s != p["a"]]
        for i, a in enumerate(order):
            if a == p["a"]:
                t.wait_ge(S["ld%d" % p["gslab"][gi]], 16)
            else:
                t.wait_ge(S["x%d_%d" % (gi, a)], p["x_expect"][gi][a])
            for k in ks:
                name, c0 = p["rhs"][k][a]
                z0 = ZP * k + 3 - a
                mm = t.matmul(T["p%d" % k][:, 0:TK], T.z[:, z0:z0 + 128], T[name][:, c0:c0 + TK],
                              i == 0, i == len(order) - 1)
                if i == len(order) - 1:
                    mm.then_inc(S["mm%d" % k], 1)

    for gi, ks in enumerate(p["groups"]):
        if not p["rsend"][gi]:
            continue
        g.wait_ge(S["cp%d" % gi], len(ks))
        fused([RemoteDMATransfer(dst_ids=[dst_id(d)], dma_engine_mask=mask, remote_sem=S[sem],
                                 src=T.res[:, TK * k:TK * k + TK], dst=T[buf][slot])
               for d, k, buf, slot, sem, mask in p["rsend"][gi]], [o[5] for o in p["rsend"][gi]])

    pass_on()

    for i, s in enumerate(p["stores"]):
        q = g.sync if i in (0, 3) else g.scalar
        c0 = p["slab_col"][s]
        if p["self_res"] is not None and p["self_res"][1] == s:
            k, s_, gi = p["self_res"]
            q.wait_ge(S["cp%d" % gi], len(p["groups"][gi]))
            q.dma_start(T.y[:, c0:c0 + slab], T.res[:, TK * k:TK * k + TK]).then_inc(S.st, 16)
        else:
            q.wait_ge(S["y%d" % s], p["y_expect"][s])
            q.dma_start(T.y[:, c0:c0 + slab], T.yl[s]).then_inc(S.st, 16)

    g.wait_ge(S.sent, sent[0])
    g.wait_ge(S.st, 16 * len(p["stores"]))
